import numpy as np
import ml_dtypes


def mxq(x, axis, fmt="e4m3"):
    dtype, down = {"e4m3": (ml_dtypes.float8_e4m3fn, 7), "e5m2": (ml_dtypes.float8_e5m2, 14)}[fmt]
    v = np.moveaxis(np.asarray(x, np.float32).astype(ml_dtypes.bfloat16).astype(np.float64), axis, -1)
    blocks = v.reshape(v.shape[:-1] + (-1, 32))
    amax = np.abs(blocks).max(-1, keepdims=True)
    byte = np.maximum(np.where(amax > 0, np.frexp(amax)[1] - 1 + 127, 0) - down, 1)
    scale = np.exp2(byte - 127.0)
    codes = (blocks / scale).astype(np.float32).astype(dtype).astype(np.float64)
    return np.moveaxis((codes * scale).reshape(v.shape), -1, axis)


WIDE = False


def mx_kscale(k):
    if not WIDE:
        return np.ones(k)
    levels = np.array([10, -10, 5, -5, 0])
    if k % 512:
        return np.exp2(np.random.permutation(np.resize(levels, k // 32))).repeat(32)
    a = np.empty((k // 512, 16))
    for p in range(k // 512):
        a[p, :8] = np.random.permutation(np.resize(levels, 8))
        for g in range(8):
            far = levels[np.abs(levels - a[p, g]) >= 10]
            a[p, g + 8] = far[np.random.randint(len(far))]
    return np.exp2(a.ravel()).repeat(32)


def f64(x):
    return np.asarray(x).astype(np.float64)


def striped8(idx):
    return np.asarray(idx).reshape(8, -1, 16).transpose(0, 2, 1).reshape(128, -1).astype(np.uint16)


def unstriped8(offs):
    return offs.reshape(8, 16, -1).transpose(0, 2, 1).reshape(8, -1).astype(np.int64)


def pick8(x, idx, run):
    r = np.arange(len(x))
    return x[r[:, None], idx[r % (8 * run) // run]]


E2M1 = np.array([0.0, 0.5, 1.0, 1.5, 2.0, 3.0, 4.0, 6.0, -0.0, -0.5, -1.0, -1.5, -2.0, -3.0, -4.0, -6.0])


def pack_weight(w, fmt):
    k, n = w.shape
    w = f64(np.asarray(w, np.float32).astype(ml_dtypes.bfloat16)).reshape(k // 32, 32, n)
    amax = np.abs(w).max(1)
    if fmt == "e4m3":
        byte = np.frexp(amax)[1] - 1 + 127 - 7
    else:
        mant, ex = np.frexp(amax / 6.0)
        byte = np.where(mant > 0.5, ex, ex - 1) + 127
    byte = np.clip(np.where(amax > 0, byte, 1), 1, 254)
    scaled = (w * np.exp2(127.0 - byte)[:, None, :]).reshape(k, n).astype(np.float32)
    by_word = np.ascontiguousarray(scaled.reshape(k // 512, 128, 4, n).transpose(0, 1, 3, 2))
    if fmt == "e4m3":
        words = by_word.astype(ml_dtypes.float8_e4m3fn).view(np.uint8)
    else:
        c = by_word.astype(ml_dtypes.float4_e2m1fn).view(np.uint8) & 0xF
        words = (c[..., 0::2] | (c[..., 1::2] << 4)).reshape(k // 512, 128, 2 * n)
    return np.ascontiguousarray(words), np.ascontiguousarray(byte.astype(np.uint8).reshape(k // 512, 16, n))


def unpack_weight(words, scales, fmt):
    g, _, n = scales.shape
    words = np.ascontiguousarray(words).reshape(g, 128, n, -1)
    if fmt == "e4m3":
        vals = words.view(ml_dtypes.float8_e4m3fn).astype(np.float64)
    else:
        nib = np.empty((g, 128, n, 4), np.uint8)
        nib[..., 0::2] = words & 0xF
        nib[..., 1::2] = words >> 4
        vals = E2M1[nib]
    vals = vals * np.repeat(np.exp2(scales.astype(np.float64) - 127.0), 8, axis=1)[..., None]
    return vals.transpose(0, 1, 3, 2).reshape(g * 512, n)


D, T, I, Q = 512, 1024, 512, 128


def setup_inputs():
    n = np.random.standard_normal
    idx = np.stack([np.random.permutation(T)[:I] for _ in range(8)])
    idx2 = np.stack([np.random.permutation(T)[:I] for _ in range(8)])
    idx3 = np.stack([np.random.permutation(T)[:I] for _ in range(8)])
    idx4 = np.stack([np.random.permutation(T)[:I] for _ in range(8)])
    idx5 = np.stack([np.random.permutation(T)[:I] for _ in range(8)])
    fd = mx_kscale(D)
    keysp = pack_weight(n((D, T)) / fd[:, None], "e2m1")
    return {
        "query": (n((D, Q)) * 1.0 / np.sqrt(D) * fd[:, None]).astype(np.float32),
        "keys_words": keysp[0],
        "keys_scales": keysp[1],
        "lam": (np.random.uniform(0.4, 1.2, (Q, 1))).astype(np.float32),
        "offs": striped8(idx),
        "offs2": striped8(idx2),
        "offs3": striped8(idx3),
        "offs4": striped8(idx4),
        "offs5": striped8(idx5),
    }


def reference(query, keys_words, keys_scales, lam, offs, offs2, offs3, offs4, offs5):
    idx = unstriped8(offs)
    idx2 = unstriped8(offs2)
    idx3 = unstriped8(offs3)
    idx4 = unstriped8(offs4)
    idx5 = unstriped8(offs5)
    keysu = unpack_weight(keys_words, keys_scales, "e2m1")
    queryq = mxq(f64(query), 0, "e4m3")
    a = queryq.T @ keysu
    f1 = np.zeros((Q, T))
    f1[np.arange(Q)[:, None], idx2[np.arange(Q) % 128 // 16]] = pick8(a, idx, 16)
    c1 = a + f1
    f2 = np.zeros((Q, T))
    f2[np.arange(Q)[:, None], idx4[np.arange(Q) % 128 // 16]] = pick8(c1, idx3, 16)
    c2 = c1 + f2 * f64(lam)
    y = pick8(c2, idx5, 16)
    return y

@@ -1,0 +1,106 @@
+from contextlib import ExitStack
+
+import concourse.mybir as mybir
+
+D, T, I, Q = 512, 1024, 512, 128
+FLOPS = 2 * D * T * Q
+
+F32 = mybir.dt.float32
+BF16 = mybir.dt.bfloat16
+I32 = mybir.dt.int32
+U32 = mybir.dt.uint32
+U16 = mybir.dt.uint16
+U8 = mybir.dt.uint8
+FP8X4 = mybir.dt.float8_e4m3fn_x4
+FP4X4 = mybir.dt.float4_e2m1fn_x4
+COPY = mybir.ActivationFunctionType.Copy
+MULT = mybir.AluOpType.mult
+ADD = mybir.AluOpType.add
+
+P = 128
+PACK = 4
+BANK = 512
+HALF = I // 2
+LANES = 16
+PIECES = ((512, False), (256, True), (128, True), (128, False))
+
+
+def tile_attend_hops_one_kernel(tc, query, keys_words, keys_scales, lam, offs, offs2, offs3, offs4, offs5, out):
+    nc = tc.nc
+    with ExitStack() as ctx:
+        sb = ctx.enter_context(tc.tile_pool(name="sb", bufs=1))
+        ps = ctx.enter_context(tc.psum_pool(name="ps", bufs=1))
+
+        k_scales = sb.tile([P, T], U8, name="k_scales", align_bytes=64)
+        nc.vector.memset(k_scales[:].bitcast(I32), 0)
+
+        q_raw = sb.tile([P, PACK, Q], F32, name="q_raw", align_bytes=64)
+        k_words = sb.tile([P, 2 * T], U8, name="k_words", align_bytes=64)
+        nc.sync.dma_start(out=q_raw[:], in_=query.rearrange("(p j) q -> p j q", j=PACK))
+        nc.sync.dma_start(out=k_words[:].bitcast(I32), in_=keys_words[0].bitcast(I32))
+        for quad in range(4):
+            nc.sync.dma_start(
+                out=k_scales[32 * quad : 32 * quad + 4, :].bitcast(I32),
+                in_=keys_scales[0, 4 * quad : 4 * quad + 4, :].bitcast(I32),
+            )
+        lists = []
+        for n, src in enumerate((offs, offs2, offs3, offs4, offs5)):
+            held = sb.tile([P, I // LANES], U16, name="list%d" % n)
+            nc.sync.dma_start(held[:], src)
+            lists.append(held)
+        lam_col = sb.tile([P, 1], F32, name="lam_col")
+        nc.sync.dma_start(out=lam_col[:], in_=lam)
+
+        f1 = sb.tile([P, T], F32, name="f1", align_bytes=64)
+        f2 = sb.tile([P, T], F32, name="f2", align_bytes=64)
+        nc.vector.memset(f1[:], 0.0)
+        nc.vector.memset(f2[:], 0.0)
+
+        q_bf = sb.tile([P, Q, PACK], BF16, name="q_bf", align_bytes=64)
+        nc.vector.tensor_copy(out=q_bf[:], in_=q_raw[:].rearrange("p j q -> p q j"))
+        q_codes = sb.tile([P, Q], U32, name="q_codes", align_bytes=64)
+        q_scales = sb.tile([P, Q], U8, name="q_scales", align_bytes=64)
+        nc.vector.quantize_mx(out=q_codes[:].bitcast(FP8X4), scales=q_scales[:], in_=q_bf[:].rearrange("p q j -> p (q j)"))
+
+        a = sb.tile([P, T], F32, name="a", align_bytes=64)
+        t0 = 0
+        for b, (width, on_vector) in enumerate(PIECES):
+            cols = slice(t0, t0 + width)
+            acc = ps.tile([P, width], F32, name="acc%d" % b)
+            nc.tensor.matmul_mx(
+                out=acc[:],
+                lhsT=q_codes[:].bitcast(FP8X4),
+                lhsT_scale=q_scales[:],
+                rhs=k_words[:, 2 * t0 : 2 * (t0 + width)].bitcast(FP4X4),
+                rhs_scale=k_scales[:, cols],
+                start=True,
+                stop=True,
+            )
+            if on_vector:
+                nc.vector.tensor_copy(out=a[:, cols], in_=acc[:])
+            else:
+                nc.scalar.activation(a[:, cols], acc[:], COPY)
+            t0 = t0 + width
+
+        first = slice(0, HALF // LANES)
+        second = slice(HALF // LANES, I // LANES)
+
+        def look_up(window, held, name):
+            picked = sb.tile([P, I], F32, name=name, align_bytes=64)
+            nc.vector.tensor_copy(picked[:, 0:HALF], window[:].indirect(held[:, first]))
+            nc.scalar.activation(picked[:, HALF:I], window[:].indirect(held[:, second]), COPY)
+            return picked
+
+        g1 = look_up(a, lists[0], "g1")
+        nc.vector.tensor_copy(f1[:].indirect(lists[1][:]), g1[:])
+        c1 = sb.tile([P, T], F32, name="c1", align_bytes=64)
+        nc.vector.tensor_tensor(c1[:], a[:], f1[:], ADD)
+
+        g2 = look_up(c1, lists[2], "g2")
+        nc.vector.tensor_copy(f2[:].indirect(lists[3][:]), g2[:])
+        c2 = sb.tile([P, T], F32, name="c2", align_bytes=64)
+        nc.vector.scalar_tensor_tensor(c2[:], f2[:], lam_col[:], c1[:], MULT, ADD)
+
+        y = look_up(c2, lists[4], "y")
+        nc.sync.dma_start(out=out[:, 0:HALF], in_=y[:, 0:HALF])
+        nc.scalar.dma_start(out=out[:, HALF:I], in_=y[:, HALF:I])

@@ -1,6 +1,7 @@
 from contextlib import ExitStack
 
 import concourse.mybir as mybir
+from concourse.masks import make_identity
 
 D, T, I, Q = 512, 1024, 512, 128
 FLOPS = 2 * D * T * Q
@@ -22,6 +23,8 @@ PACK = 4
 BANK = 512
 HALF = I // 2
 LANES = 16
+SHARE = 704
+CAST = 88
 PIECES = ((512, False), (256, True), (128, True), (128, False))
 
 
@@ -44,25 +47,36 @@ def tile_attend_hops_one_kernel(tc, query, keys_words, keys_scales, lam, offs, o
                 in_=keys_scales[0, 4 * quad : 4 * quad + 4, :].bitcast(I32),
             )
         lists = []
-        for n, src in enumerate((offs, offs2, offs3, offs4, offs5)):
-            held = sb.tile([P, I // LANES], U16, name="list%d" % n)
-            nc.sync.dma_start(held[:], src)
-            lists.append(held)
+
+        def load_lists(sources):
+            for src in sources:
+                held = sb.tile([P, I // LANES], U16, name="list%d" % len(lists))
+                nc.sync.dma_start(held[:], src)
+                lists.append(held)
+
+        load_lists((offs, offs2))
         lam_col = sb.tile([P, 1], F32, name="lam_col")
         nc.sync.dma_start(out=lam_col[:], in_=lam)
+        load_lists((offs3, offs4, offs5))
 
         f1 = sb.tile([P, T], F32, name="f1", align_bytes=64)
-        f2 = sb.tile([P, T], F32, name="f2", align_bytes=64)
+        ident = sb.tile([P, P], F32, name="ident", align_bytes=64)
+        nc.vector.memset(ident[:], 0.0)
+        make_identity(nc, ident[:], nomemset=True)
         nc.vector.memset(f1[:], 0.0)
-        nc.vector.memset(f2[:], 0.0)
 
-        q_bf = sb.tile([P, Q, PACK], BF16, name="q_bf", align_bytes=64)
-        nc.vector.tensor_copy(out=q_bf[:], in_=q_raw[:].rearrange("p j q -> p q j"))
+        q_bf = sb.tile([P, Q, PACK], BF16, name="q_bf", tag="staged", align_bytes=64)
+        nc.vector.tensor_copy(out=q_bf[:, 0:CAST, :], in_=q_raw[:, :, 0:CAST].rearrange("p j q -> p q j"))
+        nc.scalar.copy(out=q_bf[:, CAST:Q, :], in_=q_raw[:, :, CAST:Q].rearrange("p j q -> p q j"))
         q_codes = sb.tile([P, Q], U32, name="q_codes", align_bytes=64)
         q_scales = sb.tile([P, Q], U8, name="q_scales", align_bytes=64)
         nc.vector.quantize_mx(out=q_codes[:].bitcast(FP8X4), scales=q_scales[:], in_=q_bf[:].rearrange("p q j -> p (q j)"))
 
+        f2 = sb.tile([P, T], F32, name="f2", tag="staged", align_bytes=64)
+        nc.vector.memset(f2[:], 0.0)
+
         a = sb.tile([P, T], F32, name="a", align_bytes=64)
+        banks = []
         t0 = 0
         for b, (width, on_vector) in enumerate(PIECES):
             cols = slice(t0, t0 + width)
@@ -81,25 +95,46 @@ def tile_attend_hops_one_kernel(tc, query, keys_words, keys_scales, lam, offs, o
             else:
                 nc.scalar.activation(a[:, cols], acc[:], COPY)
             t0 = t0 + width
+            banks.append(acc)
 
         first = slice(0, HALF // LANES)
         second = slice(HALF // LANES, I // LANES)
 
         def look_up(window, held, name):
-            picked = sb.tile([P, I], F32, name=name, align_bytes=64)
+            picked = sb.tile([P, I], F32, name=name, tag=name, align_bytes=64)
             nc.vector.tensor_copy(picked[:, 0:HALF], window[:].indirect(held[:, first]))
             nc.scalar.activation(picked[:, HALF:I], window[:].indirect(held[:, second]), COPY)
             return picked
 
+        def add(total, in_psum, in_sbuf, placed):
+            nc.gpsimd.tensor_tensor(total[:, SHARE:T], in_sbuf[:, SHARE:T], placed[:, SHARE:T], ADD)
+            nc.vector.tensor_tensor(total[:, 0:BANK], in_psum[0][:], placed[:, 0:BANK], ADD)
+            nc.vector.tensor_tensor(total[:, BANK:SHARE], in_psum[1][:, 0 : SHARE - BANK], placed[:, BANK:SHARE], ADD)
+
         g1 = look_up(a, lists[0], "g1")
         nc.vector.tensor_copy(f1[:].indirect(lists[1][:]), g1[:])
+        lam_wide = sb.tile([P, I], F32, name="lam_wide", tag="g1", align_bytes=64)
+        nc.scalar.copy(out=lam_wide[:], in_=lam_col[:].to_broadcast([P, I]))
         c1 = sb.tile([P, T], F32, name="c1", align_bytes=64)
-        nc.vector.tensor_tensor(c1[:], a[:], f1[:], ADD)
+        add(c1, banks, a, f1)
 
         g2 = look_up(c1, lists[2], "g2")
-        nc.vector.tensor_copy(f2[:].indirect(lists[3][:]), g2[:])
+        c1_banks = []
+        for b, blocks in enumerate((4, 2)):
+            turned_ps = ps.tile([P, blocks * P], F32, name="turned_ps%d" % b)
+            for k in range(blocks):
+                t0 = BANK * b + P * k
+                nc.tensor.transpose(turned_ps[:, P * k : P * (k + 1)], c1[:, t0 : t0 + P], ident[:])
+            turned = sb.tile([P, blocks * P], F32, name="turned%d" % b, align_bytes=64)
+            nc.scalar.copy(out=turned[:], in_=turned_ps[:])
+            back = ps.tile([P, blocks * P], F32, name="back%d" % b)
+            for k in range(blocks):
+                nc.tensor.transpose(back[:, P * k : P * (k + 1)], turned[:, P * k : P * (k + 1)], ident[:])
+            c1_banks.append(back)
+
+        nc.vector.tensor_tensor(f2[:].indirect(lists[3][:]), g2[:], lam_wide[:], MULT)
         c2 = sb.tile([P, T], F32, name="c2", align_bytes=64)
-        nc.vector.scalar_tensor_tensor(c2[:], f2[:], lam_col[:], c1[:], MULT, ADD)
+        add(c2, c1_banks, c1, f2)
 
         y = look_up(c2, lists[4], "y")
         nc.sync.dma_start(out=out[:, 0:HALF], in_=y[:, 0:HALF])

@@ -23,7 +23,7 @@ PACK = 4
 BANK = 512
 HALF = I // 2
 LANES = 16
-SHARE = 704
+SHARE = 640
 CAST = 88
 PIECES = ((512, False), (256, True), (128, True), (128, False))
 
@@ -38,14 +38,15 @@ def tile_attend_hops_one_kernel(tc, query, keys_words, keys_scales, lam, offs, o
         nc.vector.memset(k_scales[:].bitcast(I32), 0)
 
         q_raw = sb.tile([P, PACK, Q], F32, name="q_raw", align_bytes=64)
-        k_words = sb.tile([P, 2 * T], U8, name="k_words", align_bytes=64)
+        k_words = [sb.tile([P, 2 * BANK], U8, name="k_words%d" % h, align_bytes=64) for h in range(2)]
         nc.sync.dma_start(out=q_raw[:], in_=query.rearrange("(p j) q -> p j q", j=PACK))
-        nc.sync.dma_start(out=k_words[:].bitcast(I32), in_=keys_words[0].bitcast(I32))
+        nc.sync.dma_start(out=k_words[0][:].bitcast(I32), in_=keys_words[0, :, 0 : 2 * BANK].bitcast(I32))
         for quad in range(4):
             nc.sync.dma_start(
                 out=k_scales[32 * quad : 32 * quad + 4, :].bitcast(I32),
                 in_=keys_scales[0, 4 * quad : 4 * quad + 4, :].bitcast(I32),
             )
+        nc.sync.dma_start(out=k_words[1][:].bitcast(I32), in_=keys_words[0, :, 2 * BANK : 2 * T].bitcast(I32))
         lists = []
 
         def load_lists(sources):
@@ -85,7 +86,7 @@ def tile_attend_hops_one_kernel(tc, query, keys_words, keys_scales, lam, offs, o
                 out=acc[:],
                 lhsT=q_codes[:].bitcast(FP8X4),
                 lhsT_scale=q_scales[:],
-                rhs=k_words[:, 2 * t0 : 2 * (t0 + width)].bitcast(FP4X4),
+                rhs=k_words[t0 // BANK][:, 2 * (t0 % BANK) : 2 * (t0 % BANK + width)].bitcast(FP4X4),
                 rhs_scale=k_scales[:, cols],
                 start=True,
                 stop=True,
@@ -120,7 +121,7 @@ def tile_attend_hops_one_kernel(tc, query, keys_words, keys_scales, lam, offs, o
 
         g2 = look_up(c1, lists[2], "g2")
         c1_banks = []
-        for b, blocks in enumerate((4, 2)):
+        for b, blocks in enumerate((4, 1)):
             turned_ps = ps.tile([P, blocks * P], F32, name="turned_ps%d" % b)
             for k in range(blocks):
                 t0 = BANK * b + P * k

@@ -20,12 +20,18 @@ ADD = mybir.AluOpType.add
 
 P = 128
 PACK = 4
+KEY_BYTES = 2
+QUADRANT = 32
+SCALE_ROWS = 4
+BLOCKS = D // 32
 BANK = 512
+HEAD_ROWS = 16
 HALF = I // 2
-LANES = 16
-SHARE = 640
-CAST = 88
-PIECES = ((512, False), (256, True), (128, True), (128, False))
+
+SUM_SPLIT = 640
+CAST_SPLIT = 88
+SCORE_PIECES = ((512, False), (256, True), (128, True), (128, False))
+TURNED_BLOCKS = (BANK // P, (SUM_SPLIT - BANK) // P)
 
 
 def tile_attend_hops_one_kernel(tc, query, keys_words, keys_scales, lam, offs, offs2, offs3, offs4, offs5, out):
@@ -38,27 +44,33 @@ def tile_attend_hops_one_kernel(tc, query, keys_words, keys_scales, lam, offs, o
         nc.vector.memset(k_scales[:].bitcast(I32), 0)
 
         q_raw = sb.tile([P, PACK, Q], F32, name="q_raw", align_bytes=64)
-        k_words = [sb.tile([P, 2 * BANK], U8, name="k_words%d" % h, align_bytes=64) for h in range(2)]
+        k_words = [sb.tile([P, KEY_BYTES * BANK], U8, name="k_words%d" % h, align_bytes=64) for h in range(T // BANK)]
+
+        def load_words(h):
+            src = keys_words[0, :, KEY_BYTES * BANK * h : KEY_BYTES * BANK * (h + 1)]
+            nc.sync.dma_start(out=k_words[h][:].bitcast(I32), in_=src.bitcast(I32))
+
         nc.sync.dma_start(out=q_raw[:], in_=query.rearrange("(p j) q -> p j q", j=PACK))
-        nc.sync.dma_start(out=k_words[0][:].bitcast(I32), in_=keys_words[0, :, 0 : 2 * BANK].bitcast(I32))
-        for quad in range(4):
+        load_words(0)
+        for r in range(SCALE_ROWS):
             nc.sync.dma_start(
-                out=k_scales[32 * quad : 32 * quad + 4, :].bitcast(I32),
-                in_=keys_scales[0, 4 * quad : 4 * quad + 4, :].bitcast(I32),
+                out=k_scales[r:P:QUADRANT, :].bitcast(I32),
+                in_=keys_scales[0, r:BLOCKS:SCALE_ROWS, :].bitcast(I32),
             )
-        nc.sync.dma_start(out=k_words[1][:].bitcast(I32), in_=keys_words[0, :, 2 * BANK : 2 * T].bitcast(I32))
-        lists = []
+        load_words(1)
 
-        def load_lists(sources):
-            for src in sources:
-                held = sb.tile([P, I // LANES], U16, name="list%d" % len(lists))
-                nc.sync.dma_start(held[:], src)
-                lists.append(held)
+        def load_list(src, name):
+            entries = sb.tile([P, I // HEAD_ROWS], U16, name=name)
+            nc.sync.dma_start(entries[:], src)
+            return entries
 
-        load_lists((offs, offs2))
+        idx = load_list(offs, "idx")
+        idx2 = load_list(offs2, "idx2")
         lam_col = sb.tile([P, 1], F32, name="lam_col")
         nc.sync.dma_start(out=lam_col[:], in_=lam)
-        load_lists((offs3, offs4, offs5))
+        idx3 = load_list(offs3, "idx3")
+        idx4 = load_list(offs4, "idx4")
+        idx5 = load_list(offs5, "idx5")
 
         f1 = sb.tile([P, T], F32, name="f1", align_bytes=64)
         ident = sb.tile([P, P], F32, name="ident", align_bytes=64)
@@ -66,27 +78,28 @@ def tile_attend_hops_one_kernel(tc, query, keys_words, keys_scales, lam, offs, o
         make_identity(nc, ident[:], nomemset=True)
         nc.vector.memset(f1[:], 0.0)
 
-        q_bf = sb.tile([P, Q, PACK], BF16, name="q_bf", tag="staged", align_bytes=64)
-        nc.vector.tensor_copy(out=q_bf[:, 0:CAST, :], in_=q_raw[:, :, 0:CAST].rearrange("p j q -> p q j"))
-        nc.scalar.copy(out=q_bf[:, CAST:Q, :], in_=q_raw[:, :, CAST:Q].rearrange("p j q -> p q j"))
+        q_bf = sb.tile([P, Q, PACK], BF16, name="q_bf", tag="q_bf_then_lam_f2", align_bytes=64)
+        nc.vector.tensor_copy(out=q_bf[:, 0:CAST_SPLIT, :], in_=q_raw[:, :, 0:CAST_SPLIT].rearrange("p j q -> p q j"))
+        nc.scalar.copy(out=q_bf[:, CAST_SPLIT:Q, :], in_=q_raw[:, :, CAST_SPLIT:Q].rearrange("p j q -> p q j"))
         q_codes = sb.tile([P, Q], U32, name="q_codes", align_bytes=64)
         q_scales = sb.tile([P, Q], U8, name="q_scales", align_bytes=64)
         nc.vector.quantize_mx(out=q_codes[:].bitcast(FP8X4), scales=q_scales[:], in_=q_bf[:].rearrange("p q j -> p (q j)"))
 
-        f2 = sb.tile([P, T], F32, name="f2", tag="staged", align_bytes=64)
-        nc.vector.memset(f2[:], 0.0)
+        lam_f2 = sb.tile([P, T], F32, name="lam_f2", tag="q_bf_then_lam_f2", align_bytes=64)
+        nc.vector.memset(lam_f2[:], 0.0)
 
         a = sb.tile([P, T], F32, name="a", align_bytes=64)
-        banks = []
+        a_banks = []
         t0 = 0
-        for b, (width, on_vector) in enumerate(PIECES):
+        for b, (width, on_vector) in enumerate(SCORE_PIECES):
             cols = slice(t0, t0 + width)
+            within = t0 % BANK
             acc = ps.tile([P, width], F32, name="acc%d" % b)
             nc.tensor.matmul_mx(
                 out=acc[:],
                 lhsT=q_codes[:].bitcast(FP8X4),
                 lhsT_scale=q_scales[:],
-                rhs=k_words[t0 // BANK][:, 2 * (t0 % BANK) : 2 * (t0 % BANK + width)].bitcast(FP4X4),
+                rhs=k_words[t0 // BANK][:, KEY_BYTES * within : KEY_BYTES * (within + width)].bitcast(FP4X4),
                 rhs_scale=k_scales[:, cols],
                 start=True,
                 stop=True,
@@ -96,32 +109,32 @@ def tile_attend_hops_one_kernel(tc, query, keys_words, keys_scales, lam, offs, o
             else:
                 nc.scalar.activation(a[:, cols], acc[:], COPY)
             t0 = t0 + width
-            banks.append(acc)
+            a_banks.append(acc)
 
-        first = slice(0, HALF // LANES)
-        second = slice(HALF // LANES, I // LANES)
+        first_half = slice(0, HALF // HEAD_ROWS)
+        second_half = slice(HALF // HEAD_ROWS, I // HEAD_ROWS)
 
-        def look_up(window, held, name):
+        def look_up(window, entries, name):
             picked = sb.tile([P, I], F32, name=name, tag=name, align_bytes=64)
-            nc.vector.tensor_copy(picked[:, 0:HALF], window[:].indirect(held[:, first]))
-            nc.scalar.activation(picked[:, HALF:I], window[:].indirect(held[:, second]), COPY)
+            nc.vector.tensor_copy(picked[:, 0:HALF], window[:].indirect(entries[:, first_half]))
+            nc.scalar.activation(picked[:, HALF:I], window[:].indirect(entries[:, second_half]), COPY)
             return picked
 
-        def add(total, in_psum, in_sbuf, placed):
-            nc.gpsimd.tensor_tensor(total[:, SHARE:T], in_sbuf[:, SHARE:T], placed[:, SHARE:T], ADD)
-            nc.vector.tensor_tensor(total[:, 0:BANK], in_psum[0][:], placed[:, 0:BANK], ADD)
-            nc.vector.tensor_tensor(total[:, BANK:SHARE], in_psum[1][:, 0 : SHARE - BANK], placed[:, BANK:SHARE], ADD)
+        def add(total, base_banks, base, placed):
+            nc.gpsimd.tensor_tensor(total[:, SUM_SPLIT:T], base[:, SUM_SPLIT:T], placed[:, SUM_SPLIT:T], ADD)
+            nc.vector.tensor_tensor(total[:, 0:BANK], base_banks[0][:], placed[:, 0:BANK], ADD)
+            nc.vector.tensor_tensor(total[:, BANK:SUM_SPLIT], base_banks[1][:, 0 : SUM_SPLIT - BANK], placed[:, BANK:SUM_SPLIT], ADD)
 
-        g1 = look_up(a, lists[0], "g1")
-        nc.vector.tensor_copy(f1[:].indirect(lists[1][:]), g1[:])
-        lam_wide = sb.tile([P, I], F32, name="lam_wide", tag="g1", align_bytes=64)
+        a_picked = look_up(a, idx, "a_picked")
+        nc.vector.tensor_copy(f1[:].indirect(idx2[:]), a_picked[:])
+        lam_wide = sb.tile([P, I], F32, name="lam_wide", tag="a_picked", align_bytes=64)
         nc.scalar.copy(out=lam_wide[:], in_=lam_col[:].to_broadcast([P, I]))
         c1 = sb.tile([P, T], F32, name="c1", align_bytes=64)
-        add(c1, banks, a, f1)
+        add(c1, a_banks, a, f1)
 
-        g2 = look_up(c1, lists[2], "g2")
+        c1_picked = look_up(c1, idx3, "c1_picked")
         c1_banks = []
-        for b, blocks in enumerate((4, 1)):
+        for b, blocks in enumerate(TURNED_BLOCKS):
             turned_ps = ps.tile([P, blocks * P], F32, name="turned_ps%d" % b)
             for k in range(blocks):
                 t0 = BANK * b + P * k
@@ -133,10 +146,10 @@ def tile_attend_hops_one_kernel(tc, query, keys_words, keys_scales, lam, offs, o
                 nc.tensor.transpose(back[:, P * k : P * (k + 1)], turned[:, P * k : P * (k + 1)], ident[:])
             c1_banks.append(back)
 
-        nc.vector.tensor_tensor(f2[:].indirect(lists[3][:]), g2[:], lam_wide[:], MULT)
+        nc.vector.tensor_tensor(lam_f2[:].indirect(idx4[:]), c1_picked[:], lam_wide[:], MULT)
         c2 = sb.tile([P, T], F32, name="c2", align_bytes=64)
-        add(c2, c1_banks, c1, f2)
+        add(c2, c1_banks, c1, lam_f2)
 
-        y = look_up(c2, lists[4], "y")
+        y = look_up(c2, idx5, "y")
         nc.sync.dma_start(out=out[:, 0:HALF], in_=y[:, 0:HALF])
         nc.scalar.dma_start(out=out[:, HALF:I], in_=y[:, HALF:I])

from contextlib import ExitStack

import concourse.mybir as mybir
from concourse.masks import make_identity

D, T, I, Q = 512, 1024, 512, 128
FLOPS = 2 * D * T * Q

F32 = mybir.dt.float32
BF16 = mybir.dt.bfloat16
I32 = mybir.dt.int32
U32 = mybir.dt.uint32
U16 = mybir.dt.uint16
U8 = mybir.dt.uint8
FP8X4 = mybir.dt.float8_e4m3fn_x4
FP4X4 = mybir.dt.float4_e2m1fn_x4
COPY = mybir.ActivationFunctionType.Copy
MULT = mybir.AluOpType.mult
ADD = mybir.AluOpType.add

P = 128
PACK = 4
KEY_BYTES = 2
QUADRANT = 32
SCALE_ROWS = 4
BLOCKS = D // 32
BANK = 512
HEAD_ROWS = 16
HALF = I // 2

SUM_SPLIT = 640
CAST_SPLIT = 88
SCORE_PIECES = ((512, False), (256, True), (128, True), (128, False))
TURNED_BLOCKS = (BANK // P, (SUM_SPLIT - BANK) // P)


def tile_attend_hops_one_kernel(tc, query, keys_words, keys_scales, lam, offs, offs2, offs3, offs4, offs5, out):
    nc = tc.nc
    with ExitStack() as ctx:
        sb = ctx.enter_context(tc.tile_pool(name="sb", bufs=1))
        ps = ctx.enter_context(tc.psum_pool(name="ps", bufs=1))

        k_scales = sb.tile([P, T], U8, name="k_scales", align_bytes=64)
        nc.vector.memset(k_scales[:].bitcast(I32), 0)

        q_raw = sb.tile([P, PACK, Q], F32, name="q_raw", align_bytes=64)
        k_words = [sb.tile([P, KEY_BYTES * BANK], U8, name="k_words%d" % h, align_bytes=64) for h in range(T // BANK)]

        def load_words(h):
            src = keys_words[0, :, KEY_BYTES * BANK * h : KEY_BYTES * BANK * (h + 1)]
            nc.sync.dma_start(out=k_words[h][:].bitcast(I32), in_=src.bitcast(I32))

        nc.sync.dma_start(out=q_raw[:], in_=query.rearrange("(p j) q -> p j q", j=PACK))
        load_words(0)
        for r in range(SCALE_ROWS):
            nc.sync.dma_start(
                out=k_scales[r:P:QUADRANT, :].bitcast(I32),
                in_=keys_scales[0, r:BLOCKS:SCALE_ROWS, :].bitcast(I32),
            )
        load_words(1)

        def load_list(src, name):
            entries = sb.tile([P, I // HEAD_ROWS], U16, name=name)
            nc.sync.dma_start(entries[:], src)
            return entries

        idx = load_list(offs, "idx")
        idx2 = load_list(offs2, "idx2")
        lam_col = sb.tile([P, 1], F32, name="lam_col")
        nc.sync.dma_start(out=lam_col[:], in_=lam)
        idx3 = load_list(offs3, "idx3")
        idx4 = load_list(offs4, "idx4")
        idx5 = load_list(offs5, "idx5")

        f1 = sb.tile([P, T], F32, name="f1", align_bytes=64)
        ident = sb.tile([P, P], F32, name="ident", align_bytes=64)
        nc.vector.memset(ident[:], 0.0)
        make_identity(nc, ident[:], nomemset=True)
        nc.vector.memset(f1[:], 0.0)

        q_bf = sb.tile([P, Q, PACK], BF16, name="q_bf", tag="q_bf_then_lam_f2", align_bytes=64)
        nc.vector.tensor_copy(out=q_bf[:, 0:CAST_SPLIT, :], in_=q_raw[:, :, 0:CAST_SPLIT].rearrange("p j q -> p q j"))
        nc.scalar.copy(out=q_bf[:, CAST_SPLIT:Q, :], in_=q_raw[:, :, CAST_SPLIT:Q].rearrange("p j q -> p q j"))
        q_codes = sb.tile([P, Q], U32, name="q_codes", align_bytes=64)
        q_scales = sb.tile([P, Q], U8, name="q_scales", align_bytes=64)
        nc.vector.quantize_mx(out=q_codes[:].bitcast(FP8X4), scales=q_scales[:], in_=q_bf[:].rearrange("p q j -> p (q j)"))

        lam_f2 = sb.tile([P, T], F32, name="lam_f2", tag="q_bf_then_lam_f2", align_bytes=64)
        nc.vector.memset(lam_f2[:], 0.0)

        a = sb.tile([P, T], F32, name="a", align_bytes=64)
        a_banks = []
        t0 = 0
        for b, (width, on_vector) in enumerate(SCORE_PIECES):
            cols = slice(t0, t0 + width)
            within = t0 % BANK
            acc = ps.tile([P, width], F32, name="acc%d" % b)
            nc.tensor.matmul_mx(
                out=acc[:],
                lhsT=q_codes[:].bitcast(FP8X4),
                lhsT_scale=q_scales[:],
                rhs=k_words[t0 // BANK][:, KEY_BYTES * within : KEY_BYTES * (within + width)].bitcast(FP4X4),
                rhs_scale=k_scales[:, cols],
                start=True,
                stop=True,
            )
            if on_vector:
                nc.vector.tensor_copy(out=a[:, cols], in_=acc[:])
            else:
                nc.scalar.activation(a[:, cols], acc[:], COPY)
            t0 = t0 + width
            a_banks.append(acc)

        first_half = slice(0, HALF // HEAD_ROWS)
        second_half = slice(HALF // HEAD_ROWS, I // HEAD_ROWS)

        def look_up(window, entries, name):
            picked = sb.tile([P, I], F32, name=name, tag=name, align_bytes=64)
            nc.vector.tensor_copy(picked[:, 0:HALF], window[:].indirect(entries[:, first_half]))
            nc.scalar.activation(picked[:, HALF:I], window[:].indirect(entries[:, second_half]), COPY)
            return picked

        def add(total, base_banks, base, placed):
            nc.gpsimd.tensor_tensor(total[:, SUM_SPLIT:T], base[:, SUM_SPLIT:T], placed[:, SUM_SPLIT:T], ADD)
            nc.vector.tensor_tensor(total[:, 0:BANK], base_banks[0][:], placed[:, 0:BANK], ADD)
            nc.vector.tensor_tensor(total[:, BANK:SUM_SPLIT], base_banks[1][:, 0 : SUM_SPLIT - BANK], placed[:, BANK:SUM_SPLIT], ADD)

        a_picked = look_up(a, idx, "a_picked")
        nc.vector.tensor_copy(f1[:].indirect(idx2[:]), a_picked[:])
        lam_wide = sb.tile([P, I], F32, name="lam_wide", tag="a_picked", align_bytes=64)
        nc.scalar.copy(out=lam_wide[:], in_=lam_col[:].to_broadcast([P, I]))
        c1 = sb.tile([P, T], F32, name="c1", align_bytes=64)
        add(c1, a_banks, a, f1)

        c1_picked = look_up(c1, idx3, "c1_picked")
        c1_banks = []
        for b, blocks in enumerate(TURNED_BLOCKS):
            turned_ps = ps.tile([P, blocks * P], F32, name="turned_ps%d" % b)
            for k in range(blocks):
                t0 = BANK * b + P * k
                nc.tensor.transpose(turned_ps[:, P * k : P * (k + 1)], c1[:, t0 : t0 + P], ident[:])
            turned = sb.tile([P, blocks * P], F32, name="turned%d" % b, align_bytes=64)
            nc.scalar.copy(out=turned[:], in_=turned_ps[:])
            back = ps.tile([P, blocks * P], F32, name="back%d" % b)
            for k in range(blocks):
                nc.tensor.transpose(back[:, P * k : P * (k + 1)], turned[:, P * k : P * (k + 1)], ident[:])
            c1_banks.append(back)

        nc.vector.tensor_tensor(lam_f2[:].indirect(idx4[:]), c1_picked[:], lam_wide[:], MULT)
        c2 = sb.tile([P, T], F32, name="c2", align_bytes=64)
        add(c2, c1_banks, c1, lam_f2)

        y = look_up(c2, idx5, "y")
        nc.sync.dma_start(out=out[:, 0:HALF], in_=y[:, 0:HALF])
        nc.scalar.dma_start(out=out[:, HALF:I], in_=y[:, HALF:I])
